import numpy as np
import ml_dtypes


def mxq(x, axis, fmt="e4m3"):
    dtype, down = {"e4m3": (ml_dtypes.float8_e4m3fn, 7), "e5m2": (ml_dtypes.float8_e5m2, 14)}[fmt]
    v = np.moveaxis(np.asarray(x, np.float32).astype(ml_dtypes.bfloat16).astype(np.float64), axis, -1)
    blocks = v.reshape(v.shape[:-1] + (-1, 32))
    amax = np.abs(blocks).max(-1, keepdims=True)
    byte = np.maximum(np.where(amax > 0, np.frexp(amax)[1] - 1 + 127, 0) - down, 1)
    scale = np.exp2(byte - 127.0)
    codes = (blocks / scale).astype(np.float32).astype(dtype).astype(np.float64)
    return np.moveaxis((codes * scale).reshape(v.shape), -1, axis)


WIDE = False


def mx_kscale(k):
    if not WIDE:
        return np.ones(k)
    levels = np.array([30, -30])
    if k % 512:
        return np.exp2(np.random.permutation(np.resize(levels, k // 32))).repeat(32)
    a = np.empty((k // 512, 16))
    for p in range(k // 512):
        a[p, :8] = np.random.permutation(np.resize(levels, 8))
        for g in range(8):
            far = levels[np.abs(levels - a[p, g]) >= 10]
            a[p, g + 8] = far[np.random.randint(len(far))]
    return np.exp2(a.ravel()).repeat(32)


def f64(x):
    return np.asarray(x).astype(np.float64)


def striped(idx):
    return np.tile(idx.reshape(-1, 16).T, (8, 1)).astype(np.uint16)


def unstriped(offs):
    return offs[:16].T.reshape(-1).astype(np.int64)


def bf(x):
    return np.asarray(x, np.float32).astype(ml_dtypes.bfloat16)


E2M1 = np.array([0.0, 0.5, 1.0, 1.5, 2.0, 3.0, 4.0, 6.0, -0.0, -0.5, -1.0, -1.5, -2.0, -3.0, -4.0, -6.0])


def pack_weight(w, fmt):
    k, n = w.shape
    w = f64(bf(w)).reshape(k // 32, 32, n)
    amax = np.abs(w).max(1)
    if fmt in ("e4m3", "e5m2"):
        byte = np.frexp(amax)[1] - 1 + 127 - (7 if fmt == "e4m3" else 14)
    else:
        mant, ex = np.frexp(amax / 6.0)
        byte = np.where(mant > 0.5, ex, ex - 1) + 127
    byte = np.clip(np.where(amax > 0, byte, 1), 1, 254)
    scaled = (w * np.exp2(127.0 - byte)[:, None, :]).reshape(k, n).astype(np.float32)
    by_word = np.ascontiguousarray(scaled.reshape(k // 512, 128, 4, n).transpose(0, 1, 3, 2))
    if fmt in ("e4m3", "e5m2"):
        words = by_word.astype(ml_dtypes.float8_e4m3fn if fmt == "e4m3" else ml_dtypes.float8_e5m2).view(np.uint8)
    else:
        c = by_word.astype(ml_dtypes.float4_e2m1fn).view(np.uint8) & 0xF
        words = c[..., 0::2] | (c[..., 1::2] << 4)
    return np.ascontiguousarray(words), np.ascontiguousarray(byte.astype(np.uint8).reshape(k // 512, 16, n))


def unpack_weight(words, scales, fmt):
    g, p, n, _ = words.shape
    if fmt in ("e4m3", "e5m2"):
        vals = np.ascontiguousarray(words).view(ml_dtypes.float8_e4m3fn if fmt == "e4m3" else ml_dtypes.float8_e5m2).astype(np.float64)
    else:
        nib = np.empty((g, p, n, 4), np.uint8)
        nib[..., 0::2] = words & 0xF
        nib[..., 1::2] = words >> 4
        vals = E2M1[nib]
    vals = vals * np.repeat(np.exp2(scales.astype(np.float64) - 127.0), 8, axis=1)[..., None]
    return vals.transpose(0, 1, 3, 2).reshape(g * 512, n)


K, T, S, H, N = 1536, 2048, 1024, 1024, 512


def setup_inputs():
    n = np.random.standard_normal
    s = mx_kscale(K)[:, None]
    u = mx_kscale(H)[:, None]
    errors = n((K, T)) * np.exp(1.0 * n((1, T))) * s
    tab_words, tab_scales = pack_weight(errors, "e5m2")
    w2_words, w2_scales = pack_weight(0.5 * n((H, N)) / np.sqrt(H) / u, "e4m3")
    return {
        "tab_words": tab_words,
        "tab_scales": tab_scales,
        "offs": striped(np.random.permutation(T)[:S]),
        "w1": (n((K, H)) / np.sqrt(K) / s).astype(np.float32),
        "gain": (np.random.uniform(0.5, 1.5, H) * u[:, 0]).astype(np.float32),
        "w2_words": w2_words,
        "w2_scales": w2_scales,
    }


def reference(tab_words, tab_scales, offs, w1, gain, w2_words, w2_scales):
    v = unpack_weight(tab_words, tab_scales, "e5m2")[:, unstriped(offs)]
    w1q = mxq(f64(w1), 0, "e4m3")
    w2 = unpack_weight(w2_words, w2_scales, "e4m3")
    a = np.maximum(w1q.T @ v, 0.0)
    h = f64(gain)[:, None] * np.log(1.0 + a)
    y = w2.T @ mxq(h, 0, "e4m3")
    return np.exp(y)

@@ -1,0 +1,241 @@
+from contextlib import ExitStack
+
+import concourse.mybir as mybir
+
+K, T, S, H, N = 1536, 2048, 1024, 1024, 512
+FLOPS = 2 * K * H * S + 2 * H * N * S
+
+F32 = mybir.dt.float32
+BF16 = mybir.dt.bfloat16
+I32 = mybir.dt.int32
+U32 = mybir.dt.uint32
+U16 = mybir.dt.uint16
+U8 = mybir.dt.uint8
+E4M3 = mybir.dt.float8_e4m3fn_x4
+E5M2 = mybir.dt.float8_e5m2_x4
+ACT = mybir.ActivationFunctionType
+ALU = mybir.AluOpType
+
+P = 128
+PACK = 4
+PASS = P * PACK
+KP = K // PASS
+HP = H // PASS
+COLS = 512
+HALVES = S // COLS
+SHIFT_ROWS = 112
+SLOT = 8192
+VECTOR_RELUS = {0: (0, 1), 1: (), 2: (), 3: (0,)}
+
+
+def tile_list_cardinality_error_correction_kernel(
+    tc, tab_words, tab_scales, offs, w1, gain, w2_words, w2_scales, out
+):
+    nc = tc.nc
+    with ExitStack() as ctx:
+        keep = ctx.enter_context(tc.tile_pool(name="keep", bufs=1))
+        placed = ctx.enter_context(tc.tile_pool(name="placed", bufs=1))
+        ring = ctx.enter_context(tc.tile_pool(name="ring", bufs=2))
+        psum = ctx.enter_context(tc.psum_pool(name="psum", bufs=1))
+
+        def place(shape, dtype, name, offset):
+            return placed.tile(shape, dtype, name=name, align_bytes=64, offset=offset)
+
+        offsets = keep.tile([P, S // 16], U16, name="offsets")
+        nc.sync.dma_start(offsets[:], offs)
+
+        tab_sc = place([P, T], U8, "tab_sc", 5 * SLOT - T // 2)
+        nc.gpsimd.memset(tab_sc[:].bitcast(I32), 0)
+        warm = place([P, 32], F32, "warm", 3 * SLOT - 64)
+        nc.vector.memset(warm[:, 0:1], 1.0)
+        nc.scalar.activation(warm[:, 16:17], warm[:, 0:1], ACT.Ln)
+
+        v_sc = [keep.tile([P, S], U8, name="v_sc%d" % a, align_bytes=64) for a in range(KP)]
+        for a in range(1, KP):
+            nc.vector.memset(v_sc[a][:].bitcast(I32), 0)
+
+        def load_w1(a, b, slot):
+            raw = place([P, PACK, PASS], F32, "w1_raw%d_%d" % (a, b), slot * SLOT)
+            nc.sync.dma_start(
+                raw[:],
+                w1[PASS * a : PASS * (a + 1), PASS * b : PASS * (b + 1)].rearrange("(p j) c -> p j c", j=PACK),
+            )
+            return raw
+
+        def load_table(a):
+            words = place([P, T], U32, "tab_w%d" % a, (6 * SLOT + SLOT // 2, 2 * SLOT, 6 * SLOT)[a])
+            nc.sync.dma_start(words[:].bitcast(I32), tab_words[a].rearrange("p n i -> p (n i)").bitcast(I32))
+            return words
+
+        def quantize_w1(raw, a, b, shares):
+            codes = keep.tile([P, PASS], U32, name="w1_q%d_%d" % (a, b), align_bytes=64)
+            scales = keep.tile([P, PASS], U8, name="w1_s%d_%d" % (a, b), align_bytes=64)
+            for copy, t0, t1 in shares:
+                if (a, b) == (1, 0):
+                    rounded = place([P, PACK * PASS], BF16, "w1_bf_held", 7 * SLOT)
+                elif (a, b) == (2, 1):
+                    rounded = place([P, PACK * PASS], BF16, "w1_bf_last", 7 * SLOT)
+                else:
+                    rounded = ring.tile([P, (t1 - t0) * PASS], BF16, name="w1_bf", align_bytes=64, bufs=3)
+                copy(
+                    rounded[:].rearrange("p (t m j) -> p m j t", m=P, j=PACK),
+                    raw[:].rearrange("p j (m t) -> p m j t", t=PACK)[:, :, :, t0:t1],
+                )
+                nc.vector.quantize_mx(codes[:, P * t0 : P * t1].bitcast(E4M3), scales[:, P * t0 : P * t1], rounded[:])
+            return codes, scales
+
+        def gather_words(words, a, half):
+            if (a, half) == (0, 1):
+                picked = place([P, COLS], U32, "v_w_held", 5 * SLOT)
+            else:
+                picked = keep.tile([P, COLS], U32, name="v_w%d_%d" % (a, half), align_bytes=64)
+            cols = slice(half * COLS // 16, (half + 1) * COLS // 16)
+            nc.vector.tensor_copy(picked[:], words[:].indirect(offsets[:, cols]))
+            return picked
+
+        tables = [load_table(0)]
+        raws = [load_w1(0, 0, 1)]
+        for q in range(4):
+            nc.sync.dma_start(
+                tab_sc[32 * q : 32 * q + 4 * KP, :].bitcast(I32),
+                tab_scales[:, 4 * q : 4 * q + 4, :].bitcast(I32),
+            )
+        tables.append(load_table(1))
+        raws.append(load_w1(1, 0, 3))
+
+        v_w = {(0, 0): gather_words(tables[0], 0, 0)}
+        nc.vector.tensor_copy(v_sc[0][:], tab_sc[:].indirect(offsets[:]))
+        for a in range(1, KP):
+            nc.scalar.dma_start(
+                v_sc[a][0:SHIFT_ROWS, :].bitcast(I32),
+                v_sc[0][4 * a : 4 * a + SHIFT_ROWS, :].bitcast(I32),
+            )
+        v_w[0, 1] = gather_words(tables[0], 0, 1)
+        raws.append(load_w1(2, 0, 4))
+        tables.append(load_table(2))
+        gains = place([P, HP, PACK], F32, "gains", SLOT)
+        nc.sync.dma_start(gains[:], gain.rearrange("(b p t) -> p b t", b=HP, t=PACK))
+
+        def first_product(banks, w_q, a, half):
+            codes, scales = w_q
+            for t in (2, 3, 0, 1):
+                nc.tensor.matmul_mx(
+                    banks[t][:],
+                    lhsT=codes[:, P * t : P * (t + 1)].bitcast(E4M3),
+                    lhsT_scale=scales[:, P * t : P * (t + 1)],
+                    rhs=v_w[a, half][:].bitcast(E5M2),
+                    rhs_scale=v_sc[a][:, COLS * half : COLS * (half + 1)],
+                    start=(a == 0),
+                    stop=(a == KP - 1),
+                )
+
+        def new_banks(side, what):
+            return [
+                psum.tile([P, COLS], F32, name="%s_%d_%d" % (what, side, t), tag="bank%d_%d" % (side, t))
+                for t in range(PACK)
+            ]
+
+        def positive_part(banks, b, half):
+            positive = keep.tile([P, PACK, COLS], F32, name="pos%d_%d" % (b, half), tag="wide%d" % half)
+            for t in (2, 3, 0, 1):
+                if t in VECTOR_RELUS[2 * b + half]:
+                    nc.vector.tensor_scalar_max(positive[:, t, :], banks[t][:], 0.0)
+                else:
+                    nc.scalar.activation(positive[:, t, :], banks[t][:], ACT.Relu)
+            return positive
+
+        def log_of(positive, c0, c1):
+            logs = ring.tile([P, PACK, c1 - c0], F32, name="logs", bufs=3)
+            nc.scalar.activation(logs[:], positive[:, :, c0:c1], ACT.Ln, bias=1.0)
+            return logs
+
+        def make_h(logs, b, width, name):
+            if name == "0_0":
+                rounded = place([P, width, PACK], BF16, "h_bf_held", 7 * SLOT)
+            else:
+                rounded = ring.tile([P, width, PACK], BF16, name="h_bf", align_bytes=64)
+            nc.vector.tensor_tensor(
+                rounded[:].rearrange("p (c i) t -> p c t i", i=2),
+                logs[:].rearrange("p t (c i) -> p c t i", i=2),
+                gains[:, b, :].unsqueeze(1).unsqueeze(3).to_broadcast([P, width // 2, PACK, 2]),
+                ALU.mult,
+            )
+            codes = keep.tile([P, width], U32, name="h_q" + name, align_bytes=64)
+            scales = keep.tile([P, width], U8, name="h_s" + name, align_bytes=64)
+            nc.vector.quantize_mx(codes[:].bitcast(E4M3), scales[:], rounded[:].rearrange("p c t -> p (c t)"))
+            return codes, scales
+
+        banks = [new_banks(half, "a0") for half in range(HALVES)]
+        for a in range(KP):
+            if a == 1:
+                for half in range(HALVES):
+                    v_w[a, half] = gather_words(tables[a], a, half)
+            if a < KP - 1:
+                shares = [(nc.scalar.copy, 0, PACK)]
+            else:
+                shares = [(nc.vector.tensor_copy, 2, PACK), (nc.scalar.copy, 0, 2)]
+            w_q = quantize_w1(raws[a], a, 0, shares)
+            for half in range(HALVES):
+                if a == KP - 1:
+                    v_w[a, half] = gather_words(tables[a], a, half)
+                first_product(banks[half], w_q, a, half)
+        raws = [load_w1(a, 1, 2 + a) for a in range(KP)]
+
+        w2_w = place([P, HP, N], U32, "w2_w", 6 * SLOT)
+        nc.sync.dma_start(w2_w[:].bitcast(I32), w2_words.rearrange("a p c i -> p a (c i)").bitcast(I32))
+        w2_sc = place([P, N], U8, "w2_sc", 6 * SLOT + 4 * HP * N)
+        nc.vector.memset(w2_sc[:].bitcast(I32), 0)
+        for q in range(4):
+            nc.sync.dma_start(
+                w2_sc[32 * q : 32 * q + 4 * HP, :].bitcast(I32),
+                w2_scales[:, 4 * q : 4 * q + 4, :].bitcast(I32),
+            )
+
+        logs = [log_of(positive_part(banks[half], 0, half), 0, COLS) for half in range(HALVES)]
+        w_q = [quantize_w1(raws[a], a, 1, [(nc.vector.tensor_copy, 0, PACK)]) for a in range(KP)]
+        h_low = [make_h(logs[half], 0, COLS, "0_%d" % half) for half in range(HALVES)]
+        banks = [new_banks(half, "a1") for half in range(HALVES)]
+        for a, half in ((0, 0), (1, 0), (0, 1), (1, 1), (2, 0), (2, 1)):
+            first_product(banks[half], w_q[a], a, half)
+
+        def second_product(acc, n, parts):
+            for b, (codes, scales) in enumerate(parts):
+                nc.tensor.matmul_mx(
+                    acc,
+                    lhsT=w2_w[:, b, P * n : P * (n + 1)].bitcast(E4M3),
+                    lhsT_scale=w2_sc[4 * b : P, P * n : P * (n + 1)],
+                    rhs=codes.bitcast(E4M3),
+                    rhs_scale=scales,
+                    start=(b == 0),
+                    stop=(b == HP - 1),
+                )
+
+        logs = log_of(positive_part(banks[0], 1, 0), 0, COLS)
+        positive = positive_part(banks[1], 1, 1)
+        h_high = make_h(logs, 1, COLS, "1_0")
+        quarter = COLS // 2
+        h_last = [make_h(log_of(positive, quarter * c, quarter * (c + 1)), 1, quarter, "1_1_%d" % c) for c in range(2)]
+
+        banks = new_banks(0, "y")
+        factors = keep.tile([P, N // P, COLS], F32, name="factors0", tag="wide1")
+        for n in range(N // P):
+            second_product(banks[n][:], n, [(h_low[0][0][:], h_low[0][1][:]), (h_high[0][:], h_high[1][:])])
+            nc.scalar.activation(factors[:, n, :], banks[n][:], ACT.Exp)
+            nc.sync.dma_start(out[P * n : P * (n + 1), 0:COLS], factors[:, n, :])
+
+        banks = new_banks(1, "y")
+        factors = keep.tile([P, PACK, COLS], F32, name="factors1", tag="wide0")
+        for c in range(2):
+            cols = slice(quarter * c, quarter * (c + 1))
+            parts = [(h_low[1][0][:, cols], h_low[1][1][:, cols]), (h_last[c][0][:], h_last[c][1][:])]
+            for pair in range(2):
+                bank = banks[2 * c + pair]
+                for e in range(2):
+                    second_product(bank[:, quarter * e : quarter * (e + 1)], 2 * pair + e, parts)
+                nc.scalar.activation(factors[:, 2 * c + pair, :], bank[:], ACT.Exp)
+                nc.sync.dma_start(
+                    out[2 * P * pair : 2 * P * (pair + 1), COLS + quarter * c : COLS + quarter * (c + 1)].rearrange(
+                        "(e p) c -> p e c", e=2
+                    ),
+                    factors[:, 2 * c + pair, :].rearrange("p (e c) -> p e c", e=2),
+                )

@@ -25,7 +25,7 @@ COLS = 512
 HALVES = S // COLS
 SHIFT_ROWS = 112
 SLOT = 8192
-VECTOR_RELUS = {0: (0, 1), 1: (), 2: (), 3: (0,)}
+VECTOR_RELUS = {0: (0, 1), 1: (), 2: (), 3: (0, 1)}
 
 
 def tile_list_cardinality_error_correction_kernel(
@@ -45,7 +45,7 @@ def tile_list_cardinality_error_correction_kernel(
         nc.sync.dma_start(offsets[:], offs)
 
         tab_sc = place([P, T], U8, "tab_sc", 5 * SLOT - T // 2)
-        nc.gpsimd.memset(tab_sc[:].bitcast(I32), 0)
+        nc.vector.memset(tab_sc[:].bitcast(I32), 0)
         warm = place([P, 32], F32, "warm", 3 * SLOT - 64)
         nc.vector.memset(warm[:, 0:1], 1.0)
         nc.scalar.activation(warm[:, 16:17], warm[:, 0:1], ACT.Ln)
@@ -71,10 +71,8 @@ def tile_list_cardinality_error_correction_kernel(
             codes = keep.tile([P, PASS], U32, name="w1_q%d_%d" % (a, b), align_bytes=64)
             scales = keep.tile([P, PASS], U8, name="w1_s%d_%d" % (a, b), align_bytes=64)
             for copy, t0, t1 in shares:
-                if (a, b) == (1, 0):
-                    rounded = place([P, PACK * PASS], BF16, "w1_bf_held", 7 * SLOT)
-                elif (a, b) == (2, 1):
-                    rounded = place([P, PACK * PASS], BF16, "w1_bf_last", 7 * SLOT)
+                if (a, b) == (2, 1):
+                    rounded = place([P, PACK * PASS], BF16, "w1_bf_last", 8 * SLOT + SLOT // 4)
                 else:
                     rounded = ring.tile([P, (t1 - t0) * PASS], BF16, name="w1_bf", align_bytes=64, bufs=3)
                 copy(
@@ -94,22 +92,21 @@ def tile_list_cardinality_error_correction_kernel(
             return picked
 
         tables = [load_table(0)]
-        raws = [load_w1(0, 0, 1)]
         for q in range(4):
             nc.sync.dma_start(
-                tab_sc[32 * q : 32 * q + 4 * KP, :].bitcast(I32),
-                tab_scales[:, 4 * q : 4 * q + 4, :].bitcast(I32),
+                tab_sc[32 * q : 32 * q + 8, :].bitcast(I32),
+                tab_scales[0:2, 4 * q : 4 * q + 4, :].bitcast(I32),
             )
+        nc.sync.dma_start(tab_sc[8:24, :].bitcast(I32), tab_scales[2].bitcast(I32))
+        raws = [load_w1(0, 0, 1)]
         tables.append(load_table(1))
         raws.append(load_w1(1, 0, 3))
 
         v_w = {(0, 0): gather_words(tables[0], 0, 0)}
         nc.vector.tensor_copy(v_sc[0][:], tab_sc[:].indirect(offsets[:]))
-        for a in range(1, KP):
-            nc.scalar.dma_start(
-                v_sc[a][0:SHIFT_ROWS, :].bitcast(I32),
-                v_sc[0][4 * a : 4 * a + SHIFT_ROWS, :].bitcast(I32),
-            )
+        nc.sync.dma_start(v_sc[1][0:SHIFT_ROWS, :].bitcast(I32), v_sc[0][4 : 4 + SHIFT_ROWS, :].bitcast(I32))
+        for r in range(4):
+            nc.sync.dma_start(v_sc[2][r:P:32, :].bitcast(I32), v_sc[0][8 + r : 24 : 4, :].bitcast(I32))
         v_w[0, 1] = gather_words(tables[0], 0, 1)
         raws.append(load_w1(2, 0, 4))
         tables.append(load_table(2))
@@ -149,11 +146,8 @@ def tile_list_cardinality_error_correction_kernel(
             nc.scalar.activation(logs[:], positive[:, :, c0:c1], ACT.Ln, bias=1.0)
             return logs
 
-        def make_h(logs, b, width, name):
-            if name == "0_0":
-                rounded = place([P, width, PACK], BF16, "h_bf_held", 7 * SLOT)
-            else:
-                rounded = ring.tile([P, width, PACK], BF16, name="h_bf", align_bytes=64)
+        def make_h(logs, b, width, name, side):
+            rounded = place([P, width, PACK], BF16, "h_bf" + name, 8 * SLOT + side * SLOT // 2)
             nc.vector.tensor_tensor(
                 rounded[:].rearrange("p (c i) t -> p c t i", i=2),
                 logs[:].rearrange("p t (c i) -> p c t i", i=2),
@@ -191,12 +185,14 @@ def tile_list_cardinality_error_correction_kernel(
                 w2_scales[:, 4 * q : 4 * q + 4, :].bitcast(I32),
             )
 
-        logs = [log_of(positive_part(banks[half], 0, half), 0, COLS) for half in range(HALVES)]
+        positives = [positive_part(banks[half], 0, half) for half in range(HALVES)]
+        logs = [log_of(positives[half], 0, COLS) for half in range(HALVES)]
         w_q = [quantize_w1(raws[a], a, 1, [(nc.vector.tensor_copy, 0, PACK)]) for a in range(KP)]
-        h_low = [make_h(logs[half], 0, COLS, "0_%d" % half) for half in range(HALVES)]
+        h_low = [make_h(logs[0], 0, COLS, "0_0", 0)]
         banks = [new_banks(half, "a1") for half in range(HALVES)]
-        for a, half in ((0, 0), (1, 0), (0, 1), (1, 1), (2, 0), (2, 1)):
-            first_product(banks[half], w_q[a], a, half)
+        for a in range(KP):
+            for half in range(HALVES):
+                first_product(banks[half], w_q[a], a, half)
 
         def second_product(acc, n, parts):
             for b, (codes, scales) in enumerate(parts):
@@ -210,11 +206,13 @@ def tile_list_cardinality_error_correction_kernel(
                     stop=(b == HP - 1),
                 )
 
-        logs = log_of(positive_part(banks[0], 1, 0), 0, COLS)
+        positive = positive_part(banks[0], 1, 0)
+        h_low.append(make_h(logs[1], 0, COLS, "0_1", 1))
+        logs = log_of(positive, 0, COLS)
         positive = positive_part(banks[1], 1, 1)
-        h_high = make_h(logs, 1, COLS, "1_0")
+        h_high = make_h(logs, 1, COLS, "1_0", 0)
         quarter = COLS // 2
-        h_last = [make_h(log_of(positive, quarter * c, quarter * (c + 1)), 1, quarter, "1_1_%d" % c) for c in range(2)]
+        h_last = [make_h(log_of(positive, quarter * c, quarter * (c + 1)), 1, quarter, "1_1_%d" % c, 1 - c) for c in range(2)]
 
         banks = new_banks(0, "y")
         factors = keep.tile([P, N // P, COLS], F32, name="factors0", tag="wide1")

@@ -70,15 +70,18 @@ def tile_list_cardinality_error_correction_kernel(
         def quantize_w1(raw, a, b, shares):
             codes = keep.tile([P, PASS], U32, name="w1_q%d_%d" % (a, b), align_bytes=64)
             scales = keep.tile([P, PASS], U8, name="w1_s%d_%d" % (a, b), align_bytes=64)
+            staged = []
             for copy, t0, t1 in shares:
-                if (a, b) == (2, 1):
-                    rounded = place([P, PACK * PASS], BF16, "w1_bf_last", 8 * SLOT + SLOT // 4)
+                if (a, b, t0) == (2, 1, 0):
+                    rounded = place([P, 2 * PASS], BF16, "w1_bf_last", 8 * SLOT + 3 * SLOT // 8)
                 else:
                     rounded = ring.tile([P, (t1 - t0) * PASS], BF16, name="w1_bf", align_bytes=64, bufs=3)
                 copy(
                     rounded[:].rearrange("p (t m j) -> p m j t", m=P, j=PACK),
                     raw[:].rearrange("p j (m t) -> p m j t", t=PACK)[:, :, :, t0:t1],
                 )
+                staged.append((rounded, t0, t1))
+            for rounded, t0, t1 in staged:
                 nc.vector.quantize_mx(codes[:, P * t0 : P * t1].bitcast(E4M3), scales[:, P * t0 : P * t1], rounded[:])
             return codes, scales
 
@@ -142,16 +145,21 @@ def tile_list_cardinality_error_correction_kernel(
             return positive
 
         def log_of(positive, c0, c1):
-            logs = ring.tile([P, PACK, c1 - c0], F32, name="logs", bufs=3)
-            nc.scalar.activation(logs[:], positive[:, :, c0:c1], ACT.Ln, bias=1.0)
+            logs = ring.tile([P, c1 - c0, PACK], F32, name="logs", bufs=3)
+            nc.scalar.activation(
+                logs[:].rearrange("p (c i) t -> p c t i", i=2),
+                positive[:, :, c0:c1].rearrange("p t (c i) -> p c t i", i=2),
+                ACT.Ln,
+                bias=1.0,
+            )
             return logs
 
         def make_h(logs, b, width, name, side):
             rounded = place([P, width, PACK], BF16, "h_bf" + name, 8 * SLOT + side * SLOT // 2)
             nc.vector.tensor_tensor(
-                rounded[:].rearrange("p (c i) t -> p c t i", i=2),
-                logs[:].rearrange("p t (c i) -> p c t i", i=2),
-                gains[:, b, :].unsqueeze(1).unsqueeze(3).to_broadcast([P, width // 2, PACK, 2]),
+                rounded[:],
+                logs[:],
+                gains[:, b, :].unsqueeze(1).to_broadcast([P, width, PACK]),
                 ALU.mult,
             )
             codes = keep.tile([P, width], U32, name="h_q" + name, align_bytes=64)
@@ -187,24 +195,23 @@ def tile_list_cardinality_error_correction_kernel(
 
         positives = [positive_part(banks[half], 0, half) for half in range(HALVES)]
         logs = [log_of(positives[half], 0, COLS) for half in range(HALVES)]
-        w_q = [quantize_w1(raws[a], a, 1, [(nc.vector.tensor_copy, 0, PACK)]) for a in range(KP)]
+        w_q = [quantize_w1(raws[a], a, 1, [(nc.vector.tensor_copy, 2, PACK), (nc.vector.tensor_copy, 0, 2)]) for a in range(KP)]
         h_low = [make_h(logs[0], 0, COLS, "0_0", 0)]
         banks = [new_banks(half, "a1") for half in range(HALVES)]
         for a in range(KP):
             for half in range(HALVES):
                 first_product(banks[half], w_q[a], a, half)
 
-        def second_product(acc, n, parts):
-            for b, (codes, scales) in enumerate(parts):
-                nc.tensor.matmul_mx(
-                    acc,
-                    lhsT=w2_w[:, b, P * n : P * (n + 1)].bitcast(E4M3),
-                    lhsT_scale=w2_sc[4 * b : P, P * n : P * (n + 1)],
-                    rhs=codes.bitcast(E4M3),
-                    rhs_scale=scales,
-                    start=(b == 0),
-                    stop=(b == HP - 1),
-                )
+        def second_product(acc, n, b, codes, scales):
+            nc.tensor.matmul_mx(
+                acc,
+                lhsT=w2_w[:, b, P * n : P * (n + 1)].bitcast(E4M3),
+                lhsT_scale=w2_sc[4 * b : P, P * n : P * (n + 1)],
+                rhs=codes.bitcast(E4M3),
+                rhs_scale=scales,
+                start=(b == 0),
+                stop=(b == HP - 1),
+            )
 
         positive = positive_part(banks[0], 1, 0)
         h_low.append(make_h(logs[1], 0, COLS, "0_1", 1))
@@ -212,12 +219,17 @@ def tile_list_cardinality_error_correction_kernel(
         positive = positive_part(banks[1], 1, 1)
         h_high = make_h(logs, 1, COLS, "1_0", 0)
         quarter = COLS // 2
-        h_last = [make_h(log_of(positive, quarter * c, quarter * (c + 1)), 1, quarter, "1_1_%d" % c, 1 - c) for c in range(2)]
+        logs = [log_of(positive, quarter * c, quarter * (c + 1)) for c in range(2)]
+        warm_exp = keep.tile([P, 1], F32, name="warm_exp")
+        nc.scalar.activation(warm_exp[:], logs[1][:, 0, 0:1], ACT.Exp)
+        h_last = [make_h(logs[c], 1, quarter, "1_1_%d" % c, 1 - c) for c in range(2)]
 
         banks = new_banks(0, "y")
         factors = keep.tile([P, N // P, COLS], F32, name="factors0", tag="wide1")
         for n in range(N // P):
-            second_product(banks[n][:], n, [(h_low[0][0][:], h_low[0][1][:]), (h_high[0][:], h_high[1][:])])
+            second_product(banks[n][:], n, 0, h_low[0][0][:], h_low[0][1][:])
+        for n in range(N // P):
+            second_product(banks[n][:], n, 1, h_high[0][:], h_high[1][:])
             nc.scalar.activation(factors[:, n, :], banks[n][:], ACT.Exp)
             nc.sync.dma_start(out[P * n : P * (n + 1), 0:COLS], factors[:, n, :])
 
@@ -229,7 +241,8 @@ def tile_list_cardinality_error_correction_kernel(
             for pair in range(2):
                 bank = banks[2 * c + pair]
                 for e in range(2):
-                    second_product(bank[:, quarter * e : quarter * (e + 1)], 2 * pair + e, parts)
+                    for b in range(HP):
+                        second_product(bank[:, quarter * e : quarter * (e + 1)], 2 * pair + e, b, *parts[b])
                 nc.scalar.activation(factors[:, 2 * c + pair, :], bank[:], ACT.Exp)
                 nc.sync.dma_start(
                     out[2 * P * pair : 2 * P * (pair + 1), COLS + quarter * c : COLS + quarter * (c + 1)].rearrange(

@@ -23,7 +23,6 @@ KP = K // PASS
 HP = H // PASS
 COLS = 512
 HALVES = S // COLS
-SHIFT_ROWS = 112
 SLOT = 8192
 VECTOR_RELUS = {0: (0, 1), 1: (), 2: (), 3: (0, 1)}
 
@@ -44,18 +43,18 @@ def tile_list_cardinality_error_correction_kernel(
         offsets = keep.tile([P, S // 16], U16, name="offsets")
         nc.sync.dma_start(offsets[:], offs)
 
-        tab_sc = place([P, T], U8, "tab_sc", 5 * SLOT - T // 2)
+        tab_sc = place([P, T], U8, "tab_sc", 0)
         nc.vector.memset(tab_sc[:].bitcast(I32), 0)
-        warm = place([P, 32], F32, "warm", 3 * SLOT - 64)
+        warm = keep.tile([P, 2], F32, name="warm")
         nc.vector.memset(warm[:, 0:1], 1.0)
-        nc.scalar.activation(warm[:, 16:17], warm[:, 0:1], ACT.Ln)
+        nc.scalar.activation(warm[:, 1:2], warm[:, 0:1], ACT.Ln)
 
         v_sc = [keep.tile([P, S], U8, name="v_sc%d" % a, align_bytes=64) for a in range(KP)]
         for a in range(1, KP):
             nc.vector.memset(v_sc[a][:].bitcast(I32), 0)
 
-        def load_w1(a, b, slot):
-            raw = place([P, PACK, PASS], F32, "w1_raw%d_%d" % (a, b), slot * SLOT)
+        def load_w1(a, b):
+            raw = keep.tile([P, PACK, PASS], F32, name="w1_raw%d_%d" % (a, b))
             nc.sync.dma_start(
                 raw[:],
                 w1[PASS * a : PASS * (a + 1), PASS * b : PASS * (b + 1)].rearrange("(p j) c -> p j c", j=PACK),
@@ -63,7 +62,7 @@ def tile_list_cardinality_error_correction_kernel(
             return raw
 
         def load_table(a):
-            words = place([P, T], U32, "tab_w%d" % a, (6 * SLOT + SLOT // 2, 2 * SLOT, 6 * SLOT)[a])
+            words = keep.tile([P, T], U32, name="tab_w%d" % a, align_bytes=64)
             nc.sync.dma_start(words[:].bitcast(I32), tab_words[a].rearrange("p n i -> p (n i)").bitcast(I32))
             return words
 
@@ -73,7 +72,7 @@ def tile_list_cardinality_error_correction_kernel(
             staged = []
             for copy, t0, t1 in shares:
                 if (a, b, t0) == (2, 1, 0):
-                    rounded = place([P, 2 * PASS], BF16, "w1_bf_last", 8 * SLOT + 3 * SLOT // 8)
+                    rounded = place([P, 2 * PASS], BF16, "w1_bf_last", SLOT // 4 + 3 * SLOT // 8)
                 else:
                     rounded = ring.tile([P, (t1 - t0) * PASS], BF16, name="w1_bf", align_bytes=64, bufs=3)
                 copy(
@@ -87,7 +86,7 @@ def tile_list_cardinality_error_correction_kernel(
 
         def gather_words(words, a, half):
             if (a, half) == (0, 1):
-                picked = place([P, COLS], U32, "v_w_held", 5 * SLOT)
+                picked = place([P, COLS], U32, "v_w_held", 0)
             else:
                 picked = keep.tile([P, COLS], U32, name="v_w%d_%d" % (a, half), align_bytes=64)
             cols = slice(half * COLS // 16, (half + 1) * COLS // 16)
@@ -97,24 +96,28 @@ def tile_list_cardinality_error_correction_kernel(
         tables = [load_table(0)]
         for q in range(4):
             nc.sync.dma_start(
-                tab_sc[32 * q : 32 * q + 8, :].bitcast(I32),
-                tab_scales[0:2, 4 * q : 4 * q + 4, :].bitcast(I32),
+                tab_sc[32 * q : 32 * q + 4, :].bitcast(I32), tab_scales[0, 4 * q : 4 * q + 4, :].bitcast(I32)
             )
-        nc.sync.dma_start(tab_sc[8:24, :].bitcast(I32), tab_scales[2].bitcast(I32))
-        raws = [load_w1(0, 0, 1)]
+        for a in range(1, KP):
+            nc.sync.dma_start(tab_sc[32 * a - 24 : 32 * a - 8, :].bitcast(I32), tab_scales[a].bitcast(I32))
+        raws = [load_w1(0, 0)]
         tables.append(load_table(1))
-        raws.append(load_w1(1, 0, 3))
+        raws.append(load_w1(1, 0))
+        raws.append(load_w1(2, 0))
 
         v_w = {(0, 0): gather_words(tables[0], 0, 0)}
         nc.vector.tensor_copy(v_sc[0][:], tab_sc[:].indirect(offsets[:]))
-        nc.sync.dma_start(v_sc[1][0:SHIFT_ROWS, :].bitcast(I32), v_sc[0][4 : 4 + SHIFT_ROWS, :].bitcast(I32))
-        for r in range(4):
-            nc.sync.dma_start(v_sc[2][r:P:32, :].bitcast(I32), v_sc[0][8 + r : 24 : 4, :].bitcast(I32))
+
+        def place_scale_rows(a):
+            for r in range(4):
+                nc.sync.dma_start(
+                    v_sc[a][r:P:32, :].bitcast(I32), v_sc[0][32 * a - 24 + r : 32 * a - 8 : 4, :].bitcast(I32)
+                )
+
+        place_scale_rows(1)
         v_w[0, 1] = gather_words(tables[0], 0, 1)
-        raws.append(load_w1(2, 0, 4))
         tables.append(load_table(2))
-        gains = place([P, HP, PACK], F32, "gains", SLOT)
-        nc.sync.dma_start(gains[:], gain.rearrange("(b p t) -> p b t", b=HP, t=PACK))
+        place_scale_rows(2)
 
         def first_product(banks, w_q, a, half):
             codes, scales = w_q
@@ -155,7 +158,7 @@ def tile_list_cardinality_error_correction_kernel(
             return logs
 
         def make_h(logs, b, width, name, side):
-            rounded = place([P, width, PACK], BF16, "h_bf" + name, 8 * SLOT + side * SLOT // 2)
+            rounded = place([P, width, PACK], BF16, "h_bf" + name, SLOT // 4 + side * SLOT // 2)
             nc.vector.tensor_tensor(
                 rounded[:],
                 logs[:],
@@ -181,11 +184,13 @@ def tile_list_cardinality_error_correction_kernel(
                 if a == KP - 1:
                     v_w[a, half] = gather_words(tables[a], a, half)
                 first_product(banks[half], w_q, a, half)
-        raws = [load_w1(a, 1, 2 + a) for a in range(KP)]
+        raws = [load_w1(a, 1) for a in range(KP)]
+        gains = keep.tile([P, HP, PACK], F32, name="gains")
+        nc.sync.dma_start(gains[:], gain.rearrange("(b p t) -> p b t", b=HP, t=PACK))
 
-        w2_w = place([P, HP, N], U32, "w2_w", 6 * SLOT)
+        w2_w = keep.tile([P, HP, N], U32, name="w2_w", align_bytes=64)
         nc.sync.dma_start(w2_w[:].bitcast(I32), w2_words.rearrange("a p c i -> p a (c i)").bitcast(I32))
-        w2_sc = place([P, N], U8, "w2_sc", 6 * SLOT + 4 * HP * N)
+        w2_sc = keep.tile([P, N], U8, name="w2_sc", align_bytes=64)
         nc.vector.memset(w2_sc[:].bitcast(I32), 0)
         for q in range(4):
             nc.sync.dma_start(
@@ -202,15 +207,15 @@ def tile_list_cardinality_error_correction_kernel(
             for half in range(HALVES):
                 first_product(banks[half], w_q[a], a, half)
 
-        def second_product(acc, n, b, codes, scales):
+        def second_product(acc, n, b, codes, scales, start, stop):
             nc.tensor.matmul_mx(
                 acc,
                 lhsT=w2_w[:, b, P * n : P * (n + 1)].bitcast(E4M3),
                 lhsT_scale=w2_sc[4 * b : P, P * n : P * (n + 1)],
                 rhs=codes.bitcast(E4M3),
                 rhs_scale=scales,
-                start=(b == 0),
-                stop=(b == HP - 1),
+                start=start,
+                stop=stop,
             )
 
         positive = positive_part(banks[0], 1, 0)
@@ -225,24 +230,27 @@ def tile_list_cardinality_error_correction_kernel(
         h_last = [make_h(logs[c], 1, quarter, "1_1_%d" % c, 1 - c) for c in range(2)]
 
         banks = new_banks(0, "y")
+        last_banks = new_banks(1, "y")
         factors = keep.tile([P, N // P, COLS], F32, name="factors0", tag="wide1")
         for n in range(N // P):
-            second_product(banks[n][:], n, 0, h_low[0][0][:], h_low[0][1][:])
+            second_product(banks[n][:], n, 0, h_low[0][0][:], h_low[0][1][:], True, False)
+        for c in range(2):
+            cols = slice(quarter * c, quarter * (c + 1))
+            for n in range(N // P):
+                acc = last_banks[2 * c + n // 2][:, quarter * (n % 2) : quarter * (n % 2 + 1)]
+                second_product(acc, n, 0, h_low[1][0][:, cols], h_low[1][1][:, cols], n % 2 == 0, False)
         for n in range(N // P):
-            second_product(banks[n][:], n, 1, h_high[0][:], h_high[1][:])
+            second_product(banks[n][:], n, 1, h_high[0][:], h_high[1][:], False, True)
             nc.scalar.activation(factors[:, n, :], banks[n][:], ACT.Exp)
             nc.sync.dma_start(out[P * n : P * (n + 1), 0:COLS], factors[:, n, :])
 
-        banks = new_banks(1, "y")
         factors = keep.tile([P, PACK, COLS], F32, name="factors1", tag="wide0")
         for c in range(2):
-            cols = slice(quarter * c, quarter * (c + 1))
-            parts = [(h_low[1][0][:, cols], h_low[1][1][:, cols]), (h_last[c][0][:], h_last[c][1][:])]
             for pair in range(2):
-                bank = banks[2 * c + pair]
+                bank = last_banks[2 * c + pair]
                 for e in range(2):
-                    for b in range(HP):
-                        second_product(bank[:, quarter * e : quarter * (e + 1)], 2 * pair + e, b, *parts[b])
+                    acc = bank[:, quarter * e : quarter * (e + 1)]
+                    second_product(acc, 2 * pair + e, 1, h_last[c][0][:], h_last[c][1][:], False, e == 1)
                 nc.scalar.activation(factors[:, 2 * c + pair, :], bank[:], ACT.Exp)
                 nc.sync.dma_start(
                     out[2 * P * pair : 2 * P * (pair + 1), COLS + quarter * c : COLS + quarter * (c + 1)].rearrange(

from contextlib import ExitStack

import concourse.mybir as mybir

K, T, S, H, N = 1536, 2048, 1024, 1024, 512
FLOPS = 2 * K * H * S + 2 * H * N * S

F32 = mybir.dt.float32
BF16 = mybir.dt.bfloat16
I32 = mybir.dt.int32
U32 = mybir.dt.uint32
U16 = mybir.dt.uint16
U8 = mybir.dt.uint8
E4M3 = mybir.dt.float8_e4m3fn_x4
E5M2 = mybir.dt.float8_e5m2_x4
ACT = mybir.ActivationFunctionType
ALU = mybir.AluOpType

P = 128
PACK = 4
PASS = P * PACK
KP = K // PASS
HP = H // PASS
COLS = 512
HALVES = S // COLS
SLOT = 8192
VECTOR_RELUS = {0: (0, 1), 1: (), 2: (), 3: (0, 1)}


def tile_list_cardinality_error_correction_kernel(
    tc, tab_words, tab_scales, offs, w1, gain, w2_words, w2_scales, out
):
    nc = tc.nc
    with ExitStack() as ctx:
        keep = ctx.enter_context(tc.tile_pool(name="keep", bufs=1))
        placed = ctx.enter_context(tc.tile_pool(name="placed", bufs=1))
        ring = ctx.enter_context(tc.tile_pool(name="ring", bufs=2))
        psum = ctx.enter_context(tc.psum_pool(name="psum", bufs=1))

        def place(shape, dtype, name, offset):
            return placed.tile(shape, dtype, name=name, align_bytes=64, offset=offset)

        offsets = keep.tile([P, S // 16], U16, name="offsets")
        nc.sync.dma_start(offsets[:], offs)

        tab_sc = place([P, T], U8, "tab_sc", 0)
        nc.vector.memset(tab_sc[:].bitcast(I32), 0)
        warm = keep.tile([P, 2], F32, name="warm")
        nc.vector.memset(warm[:, 0:1], 1.0)
        nc.scalar.activation(warm[:, 1:2], warm[:, 0:1], ACT.Ln)

        v_sc = [keep.tile([P, S], U8, name="v_sc%d" % a, align_bytes=64) for a in range(KP)]
        for a in range(1, KP):
            nc.vector.memset(v_sc[a][:].bitcast(I32), 0)

        def load_w1(a, b):
            raw = keep.tile([P, PACK, PASS], F32, name="w1_raw%d_%d" % (a, b))
            nc.sync.dma_start(
                raw[:],
                w1[PASS * a : PASS * (a + 1), PASS * b : PASS * (b + 1)].rearrange("(p j) c -> p j c", j=PACK),
            )
            return raw

        def load_table(a):
            words = keep.tile([P, T], U32, name="tab_w%d" % a, align_bytes=64)
            nc.sync.dma_start(words[:].bitcast(I32), tab_words[a].rearrange("p n i -> p (n i)").bitcast(I32))
            return words

        def quantize_w1(raw, a, b, shares):
            codes = keep.tile([P, PASS], U32, name="w1_q%d_%d" % (a, b), align_bytes=64)
            scales = keep.tile([P, PASS], U8, name="w1_s%d_%d" % (a, b), align_bytes=64)
            staged = []
            for copy, t0, t1 in shares:
                if (a, b, t0) == (2, 1, 0):
                    rounded = place([P, 2 * PASS], BF16, "w1_bf_last", SLOT // 4 + 3 * SLOT // 8)
                else:
                    rounded = ring.tile([P, (t1 - t0) * PASS], BF16, name="w1_bf", align_bytes=64, bufs=3)
                copy(
                    rounded[:].rearrange("p (t m j) -> p m j t", m=P, j=PACK),
                    raw[:].rearrange("p j (m t) -> p m j t", t=PACK)[:, :, :, t0:t1],
                )
                staged.append((rounded, t0, t1))
            for rounded, t0, t1 in staged:
                nc.vector.quantize_mx(codes[:, P * t0 : P * t1].bitcast(E4M3), scales[:, P * t0 : P * t1], rounded[:])
            return codes, scales

        def gather_words(words, a, half):
            if (a, half) == (0, 1):
                picked = place([P, COLS], U32, "v_w_held", 0)
            else:
                picked = keep.tile([P, COLS], U32, name="v_w%d_%d" % (a, half), align_bytes=64)
            cols = slice(half * COLS // 16, (half + 1) * COLS // 16)
            nc.vector.tensor_copy(picked[:], words[:].indirect(offsets[:, cols]))
            return picked

        tables = [load_table(0)]
        for q in range(4):
            nc.sync.dma_start(
                tab_sc[32 * q : 32 * q + 4, :].bitcast(I32), tab_scales[0, 4 * q : 4 * q + 4, :].bitcast(I32)
            )
        for a in range(1, KP):
            nc.sync.dma_start(tab_sc[32 * a - 24 : 32 * a - 8, :].bitcast(I32), tab_scales[a].bitcast(I32))
        raws = [load_w1(0, 0)]
        tables.append(load_table(1))
        raws.append(load_w1(1, 0))
        raws.append(load_w1(2, 0))

        v_w = {(0, 0): gather_words(tables[0], 0, 0)}
        nc.vector.tensor_copy(v_sc[0][:], tab_sc[:].indirect(offsets[:]))

        def place_scale_rows(a):
            for r in range(4):
                nc.sync.dma_start(
                    v_sc[a][r:P:32, :].bitcast(I32), v_sc[0][32 * a - 24 + r : 32 * a - 8 : 4, :].bitcast(I32)
                )

        place_scale_rows(1)
        v_w[0, 1] = gather_words(tables[0], 0, 1)
        tables.append(load_table(2))
        place_scale_rows(2)

        def first_product(banks, w_q, a, half):
            codes, scales = w_q
            for t in (2, 3, 0, 1):
                nc.tensor.matmul_mx(
                    banks[t][:],
                    lhsT=codes[:, P * t : P * (t + 1)].bitcast(E4M3),
                    lhsT_scale=scales[:, P * t : P * (t + 1)],
                    rhs=v_w[a, half][:].bitcast(E5M2),
                    rhs_scale=v_sc[a][:, COLS * half : COLS * (half + 1)],
                    start=(a == 0),
                    stop=(a == KP - 1),
                )

        def new_banks(side, what):
            return [
                psum.tile([P, COLS], F32, name="%s_%d_%d" % (what, side, t), tag="bank%d_%d" % (side, t))
                for t in range(PACK)
            ]

        def positive_part(banks, b, half):
            positive = keep.tile([P, PACK, COLS], F32, name="pos%d_%d" % (b, half), tag="wide%d" % half)
            for t in (2, 3, 0, 1):
                if t in VECTOR_RELUS[2 * b + half]:
                    nc.vector.tensor_scalar_max(positive[:, t, :], banks[t][:], 0.0)
                else:
                    nc.scalar.activation(positive[:, t, :], banks[t][:], ACT.Relu)
            return positive

        def log_of(positive, c0, c1):
            logs = ring.tile([P, c1 - c0, PACK], F32, name="logs", bufs=3)
            nc.scalar.activation(
                logs[:].rearrange("p (c i) t -> p c t i", i=2),
                positive[:, :, c0:c1].rearrange("p t (c i) -> p c t i", i=2),
                ACT.Ln,
                bias=1.0,
            )
            return logs

        def make_h(logs, b, width, name, side):
            rounded = place([P, width, PACK], BF16, "h_bf" + name, SLOT // 4 + side * SLOT // 2)
            nc.vector.tensor_tensor(
                rounded[:],
                logs[:],
                gains[:, b, :].unsqueeze(1).to_broadcast([P, width, PACK]),
                ALU.mult,
            )
            codes = keep.tile([P, width], U32, name="h_q" + name, align_bytes=64)
            scales = keep.tile([P, width], U8, name="h_s" + name, align_bytes=64)
            nc.vector.quantize_mx(codes[:].bitcast(E4M3), scales[:], rounded[:].rearrange("p c t -> p (c t)"))
            return codes, scales

        banks = [new_banks(half, "a0") for half in range(HALVES)]
        for a in range(KP):
            if a == 1:
                for half in range(HALVES):
                    v_w[a, half] = gather_words(tables[a], a, half)
            if a < KP - 1:
                shares = [(nc.scalar.copy, 0, PACK)]
            else:
                shares = [(nc.vector.tensor_copy, 2, PACK), (nc.scalar.copy, 0, 2)]
            w_q = quantize_w1(raws[a], a, 0, shares)
            for half in range(HALVES):
                if a == KP - 1:
                    v_w[a, half] = gather_words(tables[a], a, half)
                first_product(banks[half], w_q, a, half)
        raws = [load_w1(a, 1) for a in range(KP)]
        gains = keep.tile([P, HP, PACK], F32, name="gains")
        nc.sync.dma_start(gains[:], gain.rearrange("(b p t) -> p b t", b=HP, t=PACK))

        w2_w = keep.tile([P, HP, N], U32, name="w2_w", align_bytes=64)
        nc.sync.dma_start(w2_w[:].bitcast(I32), w2_words.rearrange("a p c i -> p a (c i)").bitcast(I32))
        w2_sc = keep.tile([P, N], U8, name="w2_sc", align_bytes=64)
        nc.vector.memset(w2_sc[:].bitcast(I32), 0)
        for q in range(4):
            nc.sync.dma_start(
                w2_sc[32 * q : 32 * q + 4 * HP, :].bitcast(I32),
                w2_scales[:, 4 * q : 4 * q + 4, :].bitcast(I32),
            )

        positives = [positive_part(banks[half], 0, half) for half in range(HALVES)]
        logs = [log_of(positives[half], 0, COLS) for half in range(HALVES)]
        w_q = [quantize_w1(raws[a], a, 1, [(nc.vector.tensor_copy, 2, PACK), (nc.vector.tensor_copy, 0, 2)]) for a in range(KP)]
        h_low = [make_h(logs[0], 0, COLS, "0_0", 0)]
        banks = [new_banks(half, "a1") for half in range(HALVES)]
        for a in range(KP):
            for half in range(HALVES):
                first_product(banks[half], w_q[a], a, half)

        def second_product(acc, n, b, codes, scales, start, stop):
            nc.tensor.matmul_mx(
                acc,
                lhsT=w2_w[:, b, P * n : P * (n + 1)].bitcast(E4M3),
                lhsT_scale=w2_sc[4 * b : P, P * n : P * (n + 1)],
                rhs=codes.bitcast(E4M3),
                rhs_scale=scales,
                start=start,
                stop=stop,
            )

        positive = positive_part(banks[0], 1, 0)
        h_low.append(make_h(logs[1], 0, COLS, "0_1", 1))
        logs = log_of(positive, 0, COLS)
        positive = positive_part(banks[1], 1, 1)
        h_high = make_h(logs, 1, COLS, "1_0", 0)
        quarter = COLS // 2
        logs = [log_of(positive, quarter * c, quarter * (c + 1)) for c in range(2)]
        warm_exp = keep.tile([P, 1], F32, name="warm_exp")
        nc.scalar.activation(warm_exp[:], logs[1][:, 0, 0:1], ACT.Exp)
        h_last = [make_h(logs[c], 1, quarter, "1_1_%d" % c, 1 - c) for c in range(2)]

        banks = new_banks(0, "y")
        last_banks = new_banks(1, "y")
        factors = keep.tile([P, N // P, COLS], F32, name="factors0", tag="wide1")
        for n in range(N // P):
            second_product(banks[n][:], n, 0, h_low[0][0][:], h_low[0][1][:], True, False)
        for c in range(2):
            cols = slice(quarter * c, quarter * (c + 1))
            for n in range(N // P):
                acc = last_banks[2 * c + n // 2][:, quarter * (n % 2) : quarter * (n % 2 + 1)]
                second_product(acc, n, 0, h_low[1][0][:, cols], h_low[1][1][:, cols], n % 2 == 0, False)
        for n in range(N // P):
            second_product(banks[n][:], n, 1, h_high[0][:], h_high[1][:], False, True)
            nc.scalar.activation(factors[:, n, :], banks[n][:], ACT.Exp)
            nc.sync.dma_start(out[P * n : P * (n + 1), 0:COLS], factors[:, n, :])

        factors = keep.tile([P, PACK, COLS], F32, name="factors1", tag="wide0")
        for c in range(2):
            for pair in range(2):
                bank = last_banks[2 * c + pair]
                for e in range(2):
                    acc = bank[:, quarter * e : quarter * (e + 1)]
                    second_product(acc, 2 * pair + e, 1, h_last[c][0][:], h_last[c][1][:], False, e == 1)
                nc.scalar.activation(factors[:, 2 * c + pair, :], bank[:], ACT.Exp)
                nc.sync.dma_start(
                    out[2 * P * pair : 2 * P * (pair + 1), COLS + quarter * c : COLS + quarter * (c + 1)].rearrange(
                        "(e p) c -> p e c", e=2
                    ),
                    factors[:, 2 * c + pair, :].rearrange("p (e c) -> p e c", e=2),
                )
